import numpy as np, ml_dtypes
CORES = [19,147,275,403]
N = 4
QP = 128
def setup_inputs(rng):
    return {"q": rng.standard_normal((N, 128, QP), dtype=np.float32).astype(ml_dtypes.bfloat16), "k": rng.standard_normal((N, 128, 128), dtype=np.float32).astype(ml_dtypes.bfloat16), "v": rng.standard_normal((N, 128, 128), dtype=np.float32).astype(ml_dtypes.bfloat16)}
def setup_inputs_big(rng):
    d = setup_inputs(rng)
    for k in ("q", "k", "v"): d[k] = (d[k].astype(np.float32) * 1024.0).astype(d[k].dtype)
    return d
def setup_inputs_small(rng):
    d = setup_inputs(rng)
    for k in ("q", "k", "v"): d[k] = (d[k].astype(np.float32) * (1 / 1024.0)).astype(d[k].dtype)
    return d
def setup_inputs_apart(rng):
    d = setup_inputs(rng)
    f = (10.0 ** rng.permutation(np.linspace(-1.5, 1.5, N))).astype(np.float32).reshape(N, 1, 1)
    for k in ("q", "k", "v"): d[k] = (d[k].astype(np.float32) * f).astype(d[k].dtype)
    return d
def reference(q, k, v):
    Q, K, V = q.astype(np.float64), k.astype(np.float64), v.astype(np.float64)
    y = np.zeros((N, 128, QP))
    for r in range(N):
        S = [K[j].T @ Q[r] for j in range(N)]
        m = np.max([s.max(axis=0) for s in S], axis=0)
        y[r] = sum(V[j].T @ np.maximum(S[j] - 0.5 * m, 0.0) for j in range(N))
    return {"y": y.astype(ml_dtypes.bfloat16)}

@@ -1,0 +1,138 @@
+from concourse.mybir import dt, AluOpType
+
+SCRATCH = {
+    "kvo": ("sbuf", [128, 256], "bfloat16"),
+    "kvL": ("sbuf", [128, 256], "bfloat16"),
+    "kvR": ("sbuf", [128, 256], "bfloat16"),
+    "kvD": ("sbuf", [128, 256], "bfloat16"),
+    "qs": ("sbuf", [128, 128], "bfloat16"),
+    "nhI": ("sbuf", [128, 128], "bfloat16"),
+    "pat": ("sbuf", [128, 129], "bfloat16"),
+    "dI": ("dram", [1, 128 * 129], "bfloat16"),
+    "zero": ("sbuf", [128, 128], "bfloat16"),
+    "row": ("sbuf", [128, 256], "bfloat16"),
+    "w": ("sbuf", [128, 656], "bfloat16"),
+    "p": ("sbuf", [128, 512], "bfloat16"),
+    "ys": ("sbuf", [128, 128], "bfloat16"),
+}
+for _b in range(8):
+    SCRATCH["b%d" % _b] = ("psum", [128, 512], "float32")
+
+SEMAPHORES = (["ldkv", "ldq", "aL", "aR", "aD", "sent", "fI", "fX1", "fX2", "fc", "idn", "smT", "smr", "sy", "syb", "st"]
+              + ["sST%d" % j for j in range(4)] + ["sS%d" % j for j in range(4)] + ["sP%d" % j for j in range(4)]
+              + ["sw%d" % i for i in range(12)])
+
+
+def _ring(T, topo):
+    ring = [0]
+    while len(ring) < len(T.cores):
+        ring.append([j for j in range(len(T.cores))
+                     if j not in ring and topo.may_write(T.cores[ring[-1]], T.cores[j])][0])
+    return ring
+
+
+def _engines(mask):
+    return bin(mask).count("1")
+
+
+def rank_program(g, core, T, topo):
+    rank = T.rank_of(core)
+    if rank is None:
+        return
+    s = T.sem
+    ring = _ring(T, topo)
+    at = ring.index(rank)
+    nxt = T.cores[ring[(at + 1) % len(ring)]]
+    prv = T.cores[ring[(at - 1) % len(ring)]]
+
+    g.sync.dma_start(T.kvo[:, 0:128], T.k[:]).then_inc(s.ldkv, 16)
+    g.scalar.dma_start(T.kvo[:, 128:256], T.v[:]).then_inc(s.ldkv, 16)
+    g.sync.dma_start(T.qs[:], T.q[:]).then_inc(s.ldq, 16)
+
+    def send(dst, out_ap, in_ap, sem):
+        rid, pid = topo.addr(dst, core)
+        m = topo.mask(core, dst)
+        g.remote_dma(out_ap=out_ap, in_ap=in_ap, remote_sem=sem, local_sem=s.sent, pid=pid, routing_id=rid,
+                     dma_engine_mask=m)
+        return _engines(m)
+
+    g.wait_ge(s.ldkv, 32)
+    left = send(nxt, T.kvL[:], T.kvo[:], s.aL)
+    left += send(prv, T.kvR[:], T.kvo[:], s.aR)
+    n_in_prv = _engines(topo.mask(prv, core))
+    n_in_nxt = _engines(topo.mask(nxt, core))
+    g.wait_ge(s.aL, n_in_prv)
+    left += send(nxt, T.kvD[:], T.kvL[:], s.aD)
+    g.wait_ge(s.sent, left)
+
+    V, TE = g.vector, g.tensor
+    V.memset(T.pat[:], 0.0).then_inc(s.fX1, 1)
+    V.wait_ge(s.fX1, 1)
+    V.memset(T.pat[:, 0:1], -0.5).then_inc(s.fX2, 1)
+    V.memset(T.zero[:], 0.0).then_inc(s.fc, 1)
+    V.memset(T.row[0:1, 0:128], 1.0).then_inc(s.fc, 1)
+    g.scalar.wait_ge(s.fX2, 1)
+    g.scalar.dma_start(T.dI[0, :], T.pat[:]).then_inc(s.fI, 16)
+    g.scalar.wait_ge(s.fI, 16)
+    g.scalar.dma_start(T.nhI[:], T.dI[0, 0:128 * 128]).then_inc(s.idn, 16)
+
+    blocks = [T.kvo, T.kvL, T.kvR, T.kvD]
+    bST = [T.b0, T.b1, T.b2, T.b3]
+    bS = [T.b4, T.b5, T.b6, T.b7]
+    TE.wait_ge(s.ldkv, 32)
+    TE.wait_ge(s.ldq, 16)
+    for j, (sem, n) in enumerate([(None, 0), (s.aL, n_in_prv), (s.aR, n_in_nxt), (s.aD, n_in_prv)]):
+        if sem is not None:
+            TE.wait_ge(sem, n)
+        TE.matmul(bST[j][:, 0:128], T.qs[:], blocks[j][:, 0:128], True, True).then_inc(s["sST%d" % j], 1)
+        TE.matmul(bS[j][:, 0:128], blocks[j][:, 0:128], T.qs[:], True, False)
+
+    w = T.w
+    mx = AluOpType.max
+    V.wait_ge(s.sST0, 1)
+    V.tensor_copy(w[:, 0:128], bST[0][:, 0:128]).then_inc(s.sw0, 1)
+    V.wait_ge(s.sST1, 1)
+    V.wait_ge(s.sw0, 1)
+    V.tensor_tensor(w[:, 128:256], bST[1][:, 0:128], w[:, 0:128], mx).then_inc(s.sw1, 1)
+    V.wait_ge(s.sST2, 1)
+    V.wait_ge(s.sw1, 1)
+    V.tensor_tensor(w[:, 256:384], bST[2][:, 0:128], w[:, 128:256], mx).then_inc(s.sw2, 1)
+    V.wait_ge(s.sw2, 1)
+    V.tensor_tensor(w[:, 384:448], w[:, 256:320], w[:, 320:384], mx).then_inc(s.sw3, 1)
+    V.wait_ge(s.sST3, 1)
+    V.wait_ge(s.sw3, 1)
+    V.tensor_tensor(w[:, 448:512], bST[3][:, 0:64], w[:, 384:448], mx).then_inc(s.sw4, 1)
+    V.wait_ge(s.sw4, 1)
+    V.tensor_tensor(w[:, 512:576], bST[3][:, 64:128], w[:, 448:512], mx).then_inc(s.sw5, 1)
+    src, width, dst, i = 512, 64, 576, 5
+    while width > 1:
+        V.wait_ge(s["sw%d" % i], 1)
+        width //= 2
+        i += 1
+        V.tensor_tensor(w[:, dst:dst + width], w[:, src:src + width], w[:, src + width:src + 2 * width], mx
+                        ).then_inc(s["sw%d" % i], 1)
+        src, dst = dst, dst + max(width, 8)
+    mcol = w[:, src:src + 1]
+
+    TE.wait_ge(s.idn, 16)
+    TE.wait_ge(s.fc, 2)
+    TE.wait_ge(s["sw%d" % i], 1)
+    TE.matmul(T.b0[0:1, 0:128], mcol, T.nhI[:], True, True).then_inc(s.smT, 1)
+    V.wait_ge(s.smT, 1)
+    V.tensor_copy(T.row[0:1, 128:256], T.b0[0:1, 0:128]).then_inc(s.smr, 1)
+    TE.wait_ge(s.smr, 1)
+    for j in range(4):
+        TE.matmul(bS[j][:, 0:128], T.row[0:1, 0:128], T.row[0:1, 128:256], False, True).then_inc(s["sS%d" % j], 1)
+
+    V.wait_ge(s.fc, 2)
+    for j in range(4):
+        V.wait_ge(s["sS%d" % j], 1)
+        V.tensor_tensor(T.p[:, 128 * j:128 * j + 128], bS[j][:, 0:128], T.zero[:], mx).then_inc(s["sP%d" % j], 1)
+        TE.wait_ge(s["sP%d" % j], 1)
+        mm = TE.matmul(T.b1[:, 0:128], blocks[j][:, 128:256], T.p[:, 128 * j:128 * j + 128], j == 0, j == 3)
+    mm.then_inc(s.sy, 1)
+    V.wait_ge(s.sy, 1)
+    V.tensor_copy(T.ys[:], T.b1[:, 0:128]).then_inc(s.syb, 1)
+    g.sync.wait_ge(s.syb, 1)
+    g.sync.dma_start(T.y[:], T.ys[:]).then_inc(s.st, 16)
+    g.sync.wait_ge(s.st, 16)

@@ -18,7 +18,8 @@ SCRATCH = {
 for _b in range(8):
     SCRATCH["b%d" % _b] = ("psum", [128, 512], "float32")
 
-SEMAPHORES = (["ldkv", "ldq", "aL", "aR", "aD", "sent", "fI", "fX1", "fX2", "fc", "idn", "smT", "smr", "sy", "syb", "st"]
+SEMAPHORES = (["ldk", "ldv", "ldq", "aLk", "aLv", "aRk", "aRv", "aDk", "aDv", "sent",
+               "fI", "fX1", "fX2", "fc", "idn", "smT", "smr", "sy", "syb", "st"]
               + ["sST%d" % j for j in range(4)] + ["sS%d" % j for j in range(4)] + ["sP%d" % j for j in range(4)]
               + ["sw%d" % i for i in range(12)])
 
@@ -31,8 +32,10 @@ def _ring(T, topo):
     return ring
 
 
-def _engines(mask):
-    return bin(mask).count("1")
+def _half(mask, half):
+    bits = [b for b in range(16) if mask >> b & 1]
+    n = len(bits) // 2
+    return sum(1 << b for b in bits[half * n:half * n + n]), n
 
 
 def rank_program(g, core, T, topo):
@@ -44,25 +47,31 @@ def rank_program(g, core, T, topo):
     at = ring.index(rank)
     nxt = T.cores[ring[(at + 1) % len(ring)]]
     prv = T.cores[ring[(at - 1) % len(ring)]]
+    K, W_ = slice(0, 128), slice(128, 256)
 
-    g.sync.dma_start(T.kvo[:, 0:128], T.k[:]).then_inc(s.ldkv, 16)
-    g.scalar.dma_start(T.kvo[:, 128:256], T.v[:]).then_inc(s.ldkv, 16)
+    g.sync.dma_start(T.kvo[:, K], T.k[:]).then_inc(s.ldk, 16)
+    g.scalar.dma_start(T.kvo[:, W_], T.v[:]).then_inc(s.ldv, 16)
     g.sync.dma_start(T.qs[:], T.q[:]).then_inc(s.ldq, 16)
 
     def send(dst, out_ap, in_ap, sem):
         rid, pid = topo.addr(dst, core)
-        m = topo.mask(core, dst)
+        m, n = _half(topo.mask(core, dst), 0 if dst == nxt else 1)
         g.remote_dma(out_ap=out_ap, in_ap=in_ap, remote_sem=sem, local_sem=s.sent, pid=pid, routing_id=rid,
                      dma_engine_mask=m)
-        return _engines(m)
+        return n
 
-    g.wait_ge(s.ldkv, 32)
-    left = send(nxt, T.kvL[:], T.kvo[:], s.aL)
-    left += send(prv, T.kvR[:], T.kvo[:], s.aR)
-    n_in_prv = _engines(topo.mask(prv, core))
-    n_in_nxt = _engines(topo.mask(nxt, core))
-    g.wait_ge(s.aL, n_in_prv)
-    left += send(nxt, T.kvD[:], T.kvL[:], s.aD)
+    n_p = _half(topo.mask(prv, core), 0)[1]
+    n_n = _half(topo.mask(nxt, core), 1)[1]
+    g.wait_ge(s.ldk, 16)
+    left = send(nxt, T.kvL[:, K], T.kvo[:, K], s.aLk)
+    g.wait_ge(s.ldv, 16)
+    left += send(prv, T.kvR[:, W_], T.kvo[:, W_], s.aRv)
+    left += send(prv, T.kvR[:, K], T.kvo[:, K], s.aRk)
+    left += send(nxt, T.kvL[:, W_], T.kvo[:, W_], s.aLv)
+    g.wait_ge(s.aLk, n_p)
+    left += send(nxt, T.kvD[:, K], T.kvL[:, K], s.aDk)
+    g.wait_ge(s.aRv, n_n)
+    left += send(prv, T.kvD[:, W_], T.kvR[:, W_], s.aDv)
     g.wait_ge(s.sent, left)
 
     V, TE = g.vector, g.tensor
@@ -77,15 +86,15 @@ def rank_program(g, core, T, topo):
     g.scalar.dma_start(T.nhI[:], T.dI[0, 0:128 * 128]).then_inc(s.idn, 16)
 
     blocks = [T.kvo, T.kvL, T.kvR, T.kvD]
+    k_here = [(s.ldk, 16), (s.aLk, n_p), (s.aRk, n_n), (s.aDk, n_p)]
+    v_here = [(s.ldv, 16), (s.aLv, n_p), (s.aRv, n_n), (s.aDv, n_n)]
     bST = [T.b0, T.b1, T.b2, T.b3]
     bS = [T.b4, T.b5, T.b6, T.b7]
-    TE.wait_ge(s.ldkv, 32)
     TE.wait_ge(s.ldq, 16)
-    for j, (sem, n) in enumerate([(None, 0), (s.aL, n_in_prv), (s.aR, n_in_nxt), (s.aD, n_in_prv)]):
-        if sem is not None:
-            TE.wait_ge(sem, n)
-        TE.matmul(bST[j][:, 0:128], T.qs[:], blocks[j][:, 0:128], True, True).then_inc(s["sST%d" % j], 1)
-        TE.matmul(bS[j][:, 0:128], blocks[j][:, 0:128], T.qs[:], True, False)
+    for j in range(4):
+        TE.wait_ge(k_here[j][0], k_here[j][1])
+        TE.matmul(bST[j][:, 0:128], T.qs[:], blocks[j][:, K], True, True).then_inc(s["sST%d" % j], 1)
+        TE.matmul(bS[j][:, 0:128], blocks[j][:, K], T.qs[:], True, False)
 
     w = T.w
     mx = AluOpType.max
@@ -129,7 +138,8 @@ def rank_program(g, core, T, topo):
         V.wait_ge(s["sS%d" % j], 1)
         V.tensor_tensor(T.p[:, 128 * j:128 * j + 128], bS[j][:, 0:128], T.zero[:], mx).then_inc(s["sP%d" % j], 1)
         TE.wait_ge(s["sP%d" % j], 1)
-        mm = TE.matmul(T.b1[:, 0:128], blocks[j][:, 128:256], T.p[:, 128 * j:128 * j + 128], j == 0, j == 3)
+        TE.wait_ge(v_here[j][0], v_here[j][1])
+        mm = TE.matmul(T.b1[:, 0:128], blocks[j][:, W_], T.p[:, 128 * j:128 * j + 128], j == 0, j == 3)
     mm.then_inc(s.sy, 1)
     V.wait_ge(s.sy, 1)
     V.tensor_copy(T.ys[:], T.b1[:, 0:128]).then_inc(s.syb, 1)

@@ -1,4 +1,5 @@
-from concourse.mybir import dt, AluOpType
+from concourse.bass import DstId, RemoteDMATransfer
+from concourse.mybir import dt, AluOpType, AxisListType, ActivationFunctionType
 
 SCRATCH = {
     "kvo": ("sbuf", [128, 256], "bfloat16"),
@@ -6,12 +7,12 @@ SCRATCH = {
     "kvR": ("sbuf", [128, 256], "bfloat16"),
     "kvD": ("sbuf", [128, 256], "bfloat16"),
     "qs": ("sbuf", [128, 128], "bfloat16"),
+    "nh": ("sbuf", [128, 128], "bfloat16"),
     "nhI": ("sbuf", [128, 128], "bfloat16"),
-    "pat": ("sbuf", [128, 129], "bfloat16"),
-    "dI": ("dram", [1, 128 * 129], "bfloat16"),
     "zero": ("sbuf", [128, 128], "bfloat16"),
-    "row": ("sbuf", [128, 256], "bfloat16"),
-    "w": ("sbuf", [128, 656], "bfloat16"),
+    "c": ("sbuf", [128, 4], "float32"),
+    "Z1": ("sbuf", [128, 128], "bfloat16"),
+    "Mb": ("sbuf", [128, 128], "bfloat16"),
     "p": ("sbuf", [128, 512], "bfloat16"),
     "ys": ("sbuf", [128, 128], "bfloat16"),
 }
@@ -19,9 +20,9 @@ for _b in range(8):
     SCRATCH["b%d" % _b] = ("psum", [128, 512], "float32")
 
 SEMAPHORES = (["ldk", "ldv", "ldq", "aLk", "aLv", "aRk", "aRv", "aDk", "aDv", "sent",
-               "fI", "fX1", "fX2", "fc", "idn", "smT", "smr", "sy", "syb", "st"]
+               "fh", "fz", "idn", "sZ1", "sMb", "sy", "syb", "st"]
               + ["sST%d" % j for j in range(4)] + ["sS%d" % j for j in range(4)] + ["sP%d" % j for j in range(4)]
-              + ["sw%d" % i for i in range(12)])
+              + ["sc%d" % j for j in range(4)])
 
 
 def _ring(T, topo):
@@ -32,10 +33,9 @@ def _ring(T, topo):
     return ring
 
 
-def _half(mask, half):
-    bits = [b for b in range(16) if mask >> b & 1]
-    n = len(bits) // 2
-    return sum(1 << b for b in bits[half * n:half * n + n]), n
+def _alt(mask, which):
+    bits = [b for b in range(16) if mask >> b & 1][which::2]
+    return sum(1 << b for b in bits), len(bits)
 
 
 def rank_program(g, core, T, topo):
@@ -48,42 +48,38 @@ def rank_program(g, core, T, topo):
     nxt = T.cores[ring[(at + 1) % len(ring)]]
     prv = T.cores[ring[(at - 1) % len(ring)]]
     K, W_ = slice(0, 128), slice(128, 256)
+    V, TE, ACT = g.vector, g.tensor, g.scalar
+    mx = AluOpType.max
 
     g.sync.dma_start(T.kvo[:, K], T.k[:]).then_inc(s.ldk, 16)
     g.scalar.dma_start(T.kvo[:, W_], T.v[:]).then_inc(s.ldv, 16)
     g.sync.dma_start(T.qs[:], T.q[:]).then_inc(s.ldq, 16)
 
-    def send(dst, out_ap, in_ap, sem):
+    def tr(dst, out_ap, in_ap, sem):
         rid, pid = topo.addr(dst, core)
-        m, n = _half(topo.mask(core, dst), 0 if dst == nxt else 1)
-        g.remote_dma(out_ap=out_ap, in_ap=in_ap, remote_sem=sem, local_sem=s.sent, pid=pid, routing_id=rid,
-                     dma_engine_mask=m)
-        return n
+        m, n = _alt(topo.mask(core, dst), 0 if dst == nxt else 1)
+        return RemoteDMATransfer(dst_ids=[DstId(rid=rid, pnc=pid)], dma_engine_mask=m, remote_sem=sem,
+                                 src=in_ap, dst=out_ap), n
 
-    n_p = _half(topo.mask(prv, core), 0)[1]
-    n_n = _half(topo.mask(nxt, core), 1)[1]
+    def both(a, b):
+        g.remote_dma_fused([a[0], b[0]], local_sem=s.sent)
+        return a[1] + b[1]
+
+    n_p = _alt(topo.mask(prv, core), 0)[1]
+    n_n = _alt(topo.mask(nxt, core), 1)[1]
     g.wait_ge(s.ldk, 16)
-    left = send(nxt, T.kvL[:, K], T.kvo[:, K], s.aLk)
     g.wait_ge(s.ldv, 16)
-    left += send(prv, T.kvR[:, W_], T.kvo[:, W_], s.aRv)
-    left += send(prv, T.kvR[:, K], T.kvo[:, K], s.aRk)
-    left += send(nxt, T.kvL[:, W_], T.kvo[:, W_], s.aLv)
+    left = both(tr(nxt, T.kvL[:, K], T.kvo[:, K], s.aLk), tr(prv, T.kvR[:, W_], T.kvo[:, W_], s.aRv))
+    left += both(tr(nxt, T.kvL[:, W_], T.kvo[:, W_], s.aLv), tr(prv, T.kvR[:, K], T.kvo[:, K], s.aRk))
     g.wait_ge(s.aLk, n_p)
-    left += send(nxt, T.kvD[:, K], T.kvL[:, K], s.aDk)
     g.wait_ge(s.aRv, n_n)
-    left += send(prv, T.kvD[:, W_], T.kvR[:, W_], s.aDv)
+    left += both(tr(nxt, T.kvD[:, K], T.kvL[:, K], s.aDk), tr(prv, T.kvD[:, W_], T.kvR[:, W_], s.aDv))
+    g.wait_ge(s.fh, 1)
+    g.affine_select(T.nhI[:], T.nh[:], [[-1, 128]], AluOpType.is_equal, 0.0, 0, 1).then_inc(s.idn, 1)
     g.wait_ge(s.sent, left)
 
-    V, TE = g.vector, g.tensor
-    V.memset(T.pat[:], 0.0).then_inc(s.fX1, 1)
-    V.wait_ge(s.fX1, 1)
-    V.memset(T.pat[:, 0:1], -0.5).then_inc(s.fX2, 1)
-    V.memset(T.zero[:], 0.0).then_inc(s.fc, 1)
-    V.memset(T.row[0:1, 0:128], 1.0).then_inc(s.fc, 1)
-    g.scalar.wait_ge(s.fX2, 1)
-    g.scalar.dma_start(T.dI[0, :], T.pat[:]).then_inc(s.fI, 16)
-    g.scalar.wait_ge(s.fI, 16)
-    g.scalar.dma_start(T.nhI[:], T.dI[0, 0:128 * 128]).then_inc(s.idn, 16)
+    V.memset(T.nh[:], -0.5).then_inc(s.fh, 1)
+    V.memset(T.zero[:], 0.0).then_inc(s.fz, 1)
 
     blocks = [T.kvo, T.kvL, T.kvR, T.kvD]
     k_here = [(s.ldk, 16), (s.aLk, n_p), (s.aRk, n_n), (s.aDk, n_p)]
@@ -96,53 +92,42 @@ def rank_program(g, core, T, topo):
         TE.matmul(bST[j][:, 0:128], T.qs[:], blocks[j][:, K], True, True).then_inc(s["sST%d" % j], 1)
         TE.matmul(bS[j][:, 0:128], blocks[j][:, K], T.qs[:], True, False)
 
-    w = T.w
-    mx = AluOpType.max
-    V.wait_ge(s.sST0, 1)
-    V.tensor_copy(w[:, 0:128], bST[0][:, 0:128]).then_inc(s.sw0, 1)
-    V.wait_ge(s.sST1, 1)
-    V.wait_ge(s.sw0, 1)
-    V.tensor_tensor(w[:, 128:256], bST[1][:, 0:128], w[:, 0:128], mx).then_inc(s.sw1, 1)
-    V.wait_ge(s.sST2, 1)
-    V.wait_ge(s.sw1, 1)
-    V.tensor_tensor(w[:, 256:384], bST[2][:, 0:128], w[:, 128:256], mx).then_inc(s.sw2, 1)
-    V.wait_ge(s.sw2, 1)
-    V.tensor_tensor(w[:, 384:448], w[:, 256:320], w[:, 320:384], mx).then_inc(s.sw3, 1)
-    V.wait_ge(s.sST3, 1)
-    V.wait_ge(s.sw3, 1)
-    V.tensor_tensor(w[:, 448:512], bST[3][:, 0:64], w[:, 384:448], mx).then_inc(s.sw4, 1)
-    V.wait_ge(s.sw4, 1)
-    V.tensor_tensor(w[:, 512:576], bST[3][:, 64:128], w[:, 448:512], mx).then_inc(s.sw5, 1)
-    src, width, dst, i = 512, 64, 576, 5
-    while width > 1:
-        V.wait_ge(s["sw%d" % i], 1)
-        width //= 2
-        i += 1
-        V.tensor_tensor(w[:, dst:dst + width], w[:, src:src + width], w[:, src + width:src + 2 * width], mx
-                        ).then_inc(s["sw%d" % i], 1)
-        src, dst = dst, dst + max(width, 8)
-    mcol = w[:, src:src + 1]
+    def colmax(j):
+        V.wait_ge(s["sST%d" % j], 1)
+        V.tensor_reduce(T.c[:, j:j + 1], bST[j][:, 0:128], AxisListType.X, mx).then_inc(s["sc%d" % j], 1)
 
-    TE.wait_ge(s.idn, 16)
-    TE.wait_ge(s.fc, 2)
-    TE.wait_ge(s["sw%d" % i], 1)
-    TE.matmul(T.b0[0:1, 0:128], mcol, T.nhI[:], True, True).then_inc(s.smT, 1)
-    V.wait_ge(s.smT, 1)
-    V.tensor_copy(T.row[0:1, 128:256], T.b0[0:1, 0:128]).then_inc(s.smr, 1)
-    TE.wait_ge(s.smr, 1)
-    for j in range(4):
-        TE.matmul(bS[j][:, 0:128], T.row[0:1, 0:128], T.row[0:1, 128:256], False, True).then_inc(s["sS%d" % j], 1)
+    colmax(0)
+    colmax(1)
+    V.wait_ge(s.fz, 1)
+    V.wait_ge(s.sc0, 1)
+    V.wait_ge(s.sc1, 1)
+    V.tensor_scalar(T.Z1[:], T.zero[:], T.c[:, 0:1], T.c[:, 1:2], AluOpType.add, mx).then_inc(s.sZ1, 1)
+    colmax(2)
+    colmax(3)
+    V.wait_ge(s.sZ1, 1)
+    V.wait_ge(s.sc2, 1)
+    V.wait_ge(s.sc3, 1)
+    V.tensor_scalar(T.Mb[:], T.Z1[:], T.c[:, 2:3], T.c[:, 3:4], mx, mx).then_inc(s.sMb, 1)
 
-    V.wait_ge(s.fc, 2)
+    TE.wait_ge(s.idn, 1)
+    TE.wait_ge(s.sMb, 1)
     for j in range(4):
-        V.wait_ge(s["sS%d" % j], 1)
-        V.tensor_tensor(T.p[:, 128 * j:128 * j + 128], bS[j][:, 0:128], T.zero[:], mx).then_inc(s["sP%d" % j], 1)
+        TE.matmul(bS[j][:, 0:128], T.Mb[:], T.nhI[:], False, True).then_inc(s["sS%d" % j], 1)
+
+    for j in range(4):
+        pj = T.p[:, 128 * j:128 * j + 128]
+        if j % 2 == 0:
+            V.wait_ge(s["sS%d" % j], 1)
+            V.tensor_scalar(pj, bS[j][:, 0:128], 0.0, None, mx).then_inc(s["sP%d" % j], 1)
+        else:
+            ACT.wait_ge(s["sS%d" % j], 1)
+            ACT.activation(pj, bS[j][:, 0:128], ActivationFunctionType.Relu).then_inc(s["sP%d" % j], 1)
         TE.wait_ge(s["sP%d" % j], 1)
         TE.wait_ge(v_here[j][0], v_here[j][1])
-        mm = TE.matmul(T.b1[:, 0:128], blocks[j][:, W_], T.p[:, 128 * j:128 * j + 128], j == 0, j == 3)
+        mm = TE.matmul(T.b0[:, 0:128], blocks[j][:, W_], pj, j == 0, j == 3)
     mm.then_inc(s.sy, 1)
     V.wait_ge(s.sy, 1)
-    V.tensor_copy(T.ys[:], T.b1[:, 0:128]).then_inc(s.syb, 1)
+    V.tensor_copy(T.ys[:], T.b0[:, 0:128]).then_inc(s.syb, 1)
     g.sync.wait_ge(s.syb, 1)
     g.sync.dma_start(T.y[:], T.ys[:]).then_inc(s.st, 16)
     g.sync.wait_ge(s.st, 16)

@@ -7,9 +7,9 @@ SCRATCH = {
     "kvR": ("sbuf", [128, 256], "bfloat16"),
     "kvD": ("sbuf", [128, 256], "bfloat16"),
     "qs": ("sbuf", [128, 128], "bfloat16"),
-    "nh": ("sbuf", [128, 128], "bfloat16"),
+    "ones": ("sbuf", [128, 128], "bfloat16"),
+    "R": ("sbuf", [128, 128], "bfloat16"),
     "nhI": ("sbuf", [128, 128], "bfloat16"),
-    "zero": ("sbuf", [128, 128], "bfloat16"),
     "c": ("sbuf", [128, 4], "float32"),
     "Z1": ("sbuf", [128, 128], "bfloat16"),
     "Mb": ("sbuf", [128, 128], "bfloat16"),
@@ -20,7 +20,7 @@ for _b in range(8):
     SCRATCH["b%d" % _b] = ("psum", [128, 512], "float32")
 
 SEMAPHORES = (["ldk", "ldv", "ldq", "aLk", "aLv", "aRk", "aRv", "aDk", "aDv", "sent",
-               "fh", "fz", "idn", "sZ1", "sMb", "sy", "syb", "st"]
+               "f1", "sR", "sCol", "idn", "sZ1", "sMb", "sya", "syb", "scp", "st"]
               + ["sST%d" % j for j in range(4)] + ["sS%d" % j for j in range(4)] + ["sP%d" % j for j in range(4)]
               + ["sc%d" % j for j in range(4)])
 
@@ -61,25 +61,34 @@ def rank_program(g, core, T, topo):
         return RemoteDMATransfer(dst_ids=[DstId(rid=rid, pnc=pid)], dma_engine_mask=m, remote_sem=sem,
                                  src=in_ap, dst=out_ap), n
 
-    def both(a, b):
-        g.remote_dma_fused([a[0], b[0]], local_sem=s.sent)
-        return a[1] + b[1]
+    def call(*trs):
+        g.remote_dma_fused([t[0] for t in trs], local_sem=s.sent)
+        return sum(t[1] for t in trs)
 
     n_p = _alt(topo.mask(prv, core), 0)[1]
     n_n = _alt(topo.mask(nxt, core), 1)[1]
     g.wait_ge(s.ldk, 16)
+    left = call(tr(nxt, T.kvL[:, K], T.kvo[:, K], s.aLk))
     g.wait_ge(s.ldv, 16)
-    left = both(tr(nxt, T.kvL[:, K], T.kvo[:, K], s.aLk), tr(prv, T.kvR[:, W_], T.kvo[:, W_], s.aRv))
-    left += both(tr(nxt, T.kvL[:, W_], T.kvo[:, W_], s.aLv), tr(prv, T.kvR[:, K], T.kvo[:, K], s.aRk))
+    left += call(tr(prv, T.kvR[:, W_], T.kvo[:, W_], s.aRv))
+    left += call(tr(prv, T.kvR[:, K], T.kvo[:, K], s.aRk))
     g.wait_ge(s.aLk, n_p)
+    left += call(tr(nxt, T.kvD[:, K], T.kvL[:, K], s.aDk))
     g.wait_ge(s.aRv, n_n)
-    left += both(tr(nxt, T.kvD[:, K], T.kvL[:, K], s.aDk), tr(prv, T.kvD[:, W_], T.kvR[:, W_], s.aDv))
-    g.wait_ge(s.fh, 1)
-    g.affine_select(T.nhI[:], T.nh[:], [[-1, 128]], AluOpType.is_equal, 0.0, 0, 1).then_inc(s.idn, 1)
+    left += call(tr(prv, T.kvD[:, W_], T.kvR[:, W_], s.aDv),
+                 tr(nxt, T.kvL[:, W_], T.kvo[:, W_], s.aLv))
     g.wait_ge(s.sent, left)
 
-    V.memset(T.nh[:], -0.5).then_inc(s.fh, 1)
-    V.memset(T.zero[:], 0.0).then_inc(s.fz, 1)
+    V.memset(T.ones[:], 1.0).then_inc(s.f1, 1)
+    V.wait_ge(s.f1, 1)
+    V.tensor_tensor_scan(T.R[:], T.ones[:], T.ones[:], 0.0, AluOpType.mult, AluOpType.add).then_inc(s.sR, 1)
+    TE.wait_ge(s.f1, 1)
+    TE.wait_ge(s.sR, 1)
+    TE.matmul(T.b3[:, 0:1], T.R[0:1, :], T.ones[0:1, 0:1], True, True).then_inc(s.sCol, 1)
+    V.wait_ge(s.sR, 1)
+    V.wait_ge(s.sCol, 1)
+    V.tensor_scalar(T.nhI[:], T.R[:], T.b3[:, 0:1], -0.5, AluOpType.is_equal, AluOpType.mult).then_inc(s.idn, 1)
+    TE.wait_ge(s.idn, 1)
 
     blocks = [T.kvo, T.kvL, T.kvR, T.kvD]
     k_here = [(s.ldk, 16), (s.aLk, n_p), (s.aRk, n_n), (s.aDk, n_p)]
@@ -98,10 +107,9 @@ def rank_program(g, core, T, topo):
 
     colmax(0)
     colmax(1)
-    V.wait_ge(s.fz, 1)
     V.wait_ge(s.sc0, 1)
     V.wait_ge(s.sc1, 1)
-    V.tensor_scalar(T.Z1[:], T.zero[:], T.c[:, 0:1], T.c[:, 1:2], AluOpType.add, mx).then_inc(s.sZ1, 1)
+    V.tensor_scalar(T.Z1[:], T.ones[:], T.c[:, 0:1], T.c[:, 1:2], AluOpType.mult, mx).then_inc(s.sZ1, 1)
     colmax(2)
     colmax(3)
     V.wait_ge(s.sZ1, 1)
@@ -109,14 +117,14 @@ def rank_program(g, core, T, topo):
     V.wait_ge(s.sc3, 1)
     V.tensor_scalar(T.Mb[:], T.Z1[:], T.c[:, 2:3], T.c[:, 3:4], mx, mx).then_inc(s.sMb, 1)
 
-    TE.wait_ge(s.idn, 1)
     TE.wait_ge(s.sMb, 1)
-    for j in range(4):
+    order = [0, 2, 3, 1]
+    for j in order:
         TE.matmul(bS[j][:, 0:128], T.Mb[:], T.nhI[:], False, True).then_inc(s["sS%d" % j], 1)
 
-    for j in range(4):
+    for i, j in enumerate(order):
         pj = T.p[:, 128 * j:128 * j + 128]
-        if j % 2 == 0:
+        if i % 2 == 0:
             V.wait_ge(s["sS%d" % j], 1)
             V.tensor_scalar(pj, bS[j][:, 0:128], 0.0, None, mx).then_inc(s["sP%d" % j], 1)
         else:
@@ -124,10 +132,14 @@ def rank_program(g, core, T, topo):
             ACT.activation(pj, bS[j][:, 0:128], ActivationFunctionType.Relu).then_inc(s["sP%d" % j], 1)
         TE.wait_ge(s["sP%d" % j], 1)
         TE.wait_ge(v_here[j][0], v_here[j][1])
-        mm = TE.matmul(T.b0[:, 0:128], blocks[j][:, W_], pj, j == 0, j == 3)
-    mm.then_inc(s.sy, 1)
-    V.wait_ge(s.sy, 1)
-    V.tensor_copy(T.ys[:], T.b0[:, 0:128]).then_inc(s.syb, 1)
-    g.sync.wait_ge(s.syb, 1)
+        ma = TE.matmul(T.b0[:, 0:64], blocks[j][:, W_], T.p[:, 128 * j:128 * j + 64], i == 0, i == 3)
+        mb = TE.matmul(T.b1[:, 0:64], blocks[j][:, W_], T.p[:, 128 * j + 64:128 * j + 128], i == 0, i == 3)
+    ma.then_inc(s.sya, 1)
+    mb.then_inc(s.syb, 1)
+    V.wait_ge(s.sya, 1)
+    V.tensor_copy(T.ys[:, 0:64], T.b0[:, 0:64]).then_inc(s.scp, 1)
+    ACT.wait_ge(s.syb, 1)
+    ACT.activation(T.ys[:, 64:128], T.b1[:, 0:64], ActivationFunctionType.Copy).then_inc(s.scp, 1)
+    g.sync.wait_ge(s.scp, 2)
     g.sync.dma_start(T.y[:], T.ys[:]).then_inc(s.st, 16)
     g.sync.wait_ge(s.st, 16)

from concourse.bass import DstId, RemoteDMATransfer
from concourse.mybir import dt, AluOpType, AxisListType, ActivationFunctionType

SCRATCH = {
    "kvo": ("sbuf", [128, 256], "bfloat16"),
    "kvL": ("sbuf", [128, 256], "bfloat16"),
    "kvR": ("sbuf", [128, 256], "bfloat16"),
    "kvD": ("sbuf", [128, 256], "bfloat16"),
    "qs": ("sbuf", [128, 128], "bfloat16"),
    "ones": ("sbuf", [128, 128], "bfloat16"),
    "R": ("sbuf", [128, 128], "bfloat16"),
    "nhI": ("sbuf", [128, 128], "bfloat16"),
    "c": ("sbuf", [128, 4], "float32"),
    "Z1": ("sbuf", [128, 128], "bfloat16"),
    "Mb": ("sbuf", [128, 128], "bfloat16"),
    "p": ("sbuf", [128, 512], "bfloat16"),
    "ys": ("sbuf", [128, 128], "bfloat16"),
}
for _b in range(8):
    SCRATCH["b%d" % _b] = ("psum", [128, 512], "float32")

SEMAPHORES = (["ldk", "ldv", "ldq", "aLk", "aLv", "aRk", "aRv", "aDk", "aDv", "sent",
               "f1", "sR", "sCol", "idn", "sZ1", "sMb", "sya", "syb", "scp", "st"]
              + ["sST%d" % j for j in range(4)] + ["sS%d" % j for j in range(4)] + ["sP%d" % j for j in range(4)]
              + ["sc%d" % j for j in range(4)])


def _ring(T, topo):
    ring = [0]
    while len(ring) < len(T.cores):
        ring.append([j for j in range(len(T.cores))
                     if j not in ring and topo.may_write(T.cores[ring[-1]], T.cores[j])][0])
    return ring


def _alt(mask, which):
    bits = [b for b in range(16) if mask >> b & 1][which::2]
    return sum(1 << b for b in bits), len(bits)


def rank_program(g, core, T, topo):
    rank = T.rank_of(core)
    if rank is None:
        return
    s = T.sem
    ring = _ring(T, topo)
    at = ring.index(rank)
    nxt = T.cores[ring[(at + 1) % len(ring)]]
    prv = T.cores[ring[(at - 1) % len(ring)]]
    K, W_ = slice(0, 128), slice(128, 256)
    V, TE, ACT = g.vector, g.tensor, g.scalar
    mx = AluOpType.max

    g.sync.dma_start(T.kvo[:, K], T.k[:]).then_inc(s.ldk, 16)
    g.scalar.dma_start(T.kvo[:, W_], T.v[:]).then_inc(s.ldv, 16)
    g.sync.dma_start(T.qs[:], T.q[:]).then_inc(s.ldq, 16)

    def tr(dst, out_ap, in_ap, sem):
        rid, pid = topo.addr(dst, core)
        m, n = _alt(topo.mask(core, dst), 0 if dst == nxt else 1)
        return RemoteDMATransfer(dst_ids=[DstId(rid=rid, pnc=pid)], dma_engine_mask=m, remote_sem=sem,
                                 src=in_ap, dst=out_ap), n

    def call(*trs):
        g.remote_dma_fused([t[0] for t in trs], local_sem=s.sent)
        return sum(t[1] for t in trs)

    n_p = _alt(topo.mask(prv, core), 0)[1]
    n_n = _alt(topo.mask(nxt, core), 1)[1]
    g.wait_ge(s.ldk, 16)
    left = call(tr(nxt, T.kvL[:, K], T.kvo[:, K], s.aLk))
    g.wait_ge(s.ldv, 16)
    left += call(tr(prv, T.kvR[:, W_], T.kvo[:, W_], s.aRv))
    left += call(tr(prv, T.kvR[:, K], T.kvo[:, K], s.aRk))
    g.wait_ge(s.aLk, n_p)
    left += call(tr(nxt, T.kvD[:, K], T.kvL[:, K], s.aDk))
    g.wait_ge(s.aRv, n_n)
    left += call(tr(prv, T.kvD[:, W_], T.kvR[:, W_], s.aDv),
                 tr(nxt, T.kvL[:, W_], T.kvo[:, W_], s.aLv))
    g.wait_ge(s.sent, left)

    V.memset(T.ones[:], 1.0).then_inc(s.f1, 1)
    V.wait_ge(s.f1, 1)
    V.tensor_tensor_scan(T.R[:], T.ones[:], T.ones[:], 0.0, AluOpType.mult, AluOpType.add).then_inc(s.sR, 1)
    TE.wait_ge(s.f1, 1)
    TE.wait_ge(s.sR, 1)
    TE.matmul(T.b3[:, 0:1], T.R[0:1, :], T.ones[0:1, 0:1], True, True).then_inc(s.sCol, 1)
    V.wait_ge(s.sR, 1)
    V.wait_ge(s.sCol, 1)
    V.tensor_scalar(T.nhI[:], T.R[:], T.b3[:, 0:1], -0.5, AluOpType.is_equal, AluOpType.mult).then_inc(s.idn, 1)
    TE.wait_ge(s.idn, 1)

    blocks = [T.kvo, T.kvL, T.kvR, T.kvD]
    k_here = [(s.ldk, 16), (s.aLk, n_p), (s.aRk, n_n), (s.aDk, n_p)]
    v_here = [(s.ldv, 16), (s.aLv, n_p), (s.aRv, n_n), (s.aDv, n_n)]
    bST = [T.b0, T.b1, T.b2, T.b3]
    bS = [T.b4, T.b5, T.b6, T.b7]
    TE.wait_ge(s.ldq, 16)
    for j in range(4):
        TE.wait_ge(k_here[j][0], k_here[j][1])
        TE.matmul(bST[j][:, 0:128], T.qs[:], blocks[j][:, K], True, True).then_inc(s["sST%d" % j], 1)
        TE.matmul(bS[j][:, 0:128], blocks[j][:, K], T.qs[:], True, False)

    def colmax(j):
        V.wait_ge(s["sST%d" % j], 1)
        V.tensor_reduce(T.c[:, j:j + 1], bST[j][:, 0:128], AxisListType.X, mx).then_inc(s["sc%d" % j], 1)

    colmax(0)
    colmax(1)
    V.wait_ge(s.sc0, 1)
    V.wait_ge(s.sc1, 1)
    V.tensor_scalar(T.Z1[:], T.ones[:], T.c[:, 0:1], T.c[:, 1:2], AluOpType.mult, mx).then_inc(s.sZ1, 1)
    colmax(2)
    colmax(3)
    V.wait_ge(s.sZ1, 1)
    V.wait_ge(s.sc2, 1)
    V.wait_ge(s.sc3, 1)
    V.tensor_scalar(T.Mb[:], T.Z1[:], T.c[:, 2:3], T.c[:, 3:4], mx, mx).then_inc(s.sMb, 1)

    TE.wait_ge(s.sMb, 1)
    order = [0, 2, 3, 1]
    for j in order:
        TE.matmul(bS[j][:, 0:128], T.Mb[:], T.nhI[:], False, True).then_inc(s["sS%d" % j], 1)

    for i, j in enumerate(order):
        pj = T.p[:, 128 * j:128 * j + 128]
        if i % 2 == 0:
            V.wait_ge(s["sS%d" % j], 1)
            V.tensor_scalar(pj, bS[j][:, 0:128], 0.0, None, mx).then_inc(s["sP%d" % j], 1)
        else:
            ACT.wait_ge(s["sS%d" % j], 1)
            ACT.activation(pj, bS[j][:, 0:128], ActivationFunctionType.Relu).then_inc(s["sP%d" % j], 1)
        TE.wait_ge(s["sP%d" % j], 1)
        TE.wait_ge(v_here[j][0], v_here[j][1])
        ma = TE.matmul(T.b0[:, 0:64], blocks[j][:, W_], T.p[:, 128 * j:128 * j + 64], i == 0, i == 3)
        mb = TE.matmul(T.b1[:, 0:64], blocks[j][:, W_], T.p[:, 128 * j + 64:128 * j + 128], i == 0, i == 3)
    ma.then_inc(s.sya, 1)
    mb.then_inc(s.syb, 1)
    V.wait_ge(s.sya, 1)
    V.tensor_copy(T.ys[:, 0:64], T.b0[:, 0:64]).then_inc(s.scp, 1)
    ACT.wait_ge(s.syb, 1)
    ACT.activation(T.ys[:, 64:128], T.b1[:, 0:64], ActivationFunctionType.Copy).then_inc(s.scp, 1)
    g.sync.wait_ge(s.scp, 2)
    g.sync.dma_start(T.y[:], T.ys[:]).then_inc(s.st, 16)
    g.sync.wait_ge(s.st, 16)
